import numpy as np
import ml_dtypes


def mxq(x, axis, fmt="e4m3"):
    dtype, down = {"e4m3": (ml_dtypes.float8_e4m3fn, 7), "e5m2": (ml_dtypes.float8_e5m2, 14)}[fmt]
    v = np.moveaxis(np.asarray(x, np.float32).astype(ml_dtypes.bfloat16).astype(np.float64), axis, -1)
    blocks = v.reshape(v.shape[:-1] + (-1, 32))
    amax = np.abs(blocks).max(-1, keepdims=True)
    byte = np.maximum(np.where(amax > 0, np.frexp(amax)[1] - 1 + 127, 0) - down, 1)
    scale = np.exp2(byte - 127.0)
    codes = (blocks / scale).astype(np.float32).astype(dtype).astype(np.float64)
    return np.moveaxis((codes * scale).reshape(v.shape), -1, axis)


WIDE = False


def mx_kscale(k):
    if not WIDE:
        return np.ones(k)
    levels = np.array([10, -10, 5, -5, 0])
    if k % 512:
        return np.exp2(np.random.permutation(np.resize(levels, k // 32))).repeat(32)
    a = np.empty((k // 512, 16))
    for p in range(k // 512):
        a[p, :8] = np.random.permutation(np.resize(levels, 8))
        for g in range(8):
            far = levels[np.abs(levels - a[p, g]) >= 10]
            a[p, g + 8] = far[np.random.randint(len(far))]
    return np.exp2(a.ravel()).repeat(32)


def f64(x):
    return np.asarray(x).astype(np.float64)


def striped(idx):
    return np.tile(idx.reshape(-1, 16).T, (8, 1)).astype(np.uint16)


def unstriped(offs):
    return offs[:16].T.reshape(-1).astype(np.int64)


E2M1 = np.array([0.0, 0.5, 1.0, 1.5, 2.0, 3.0, 4.0, 6.0, -0.0, -0.5, -1.0, -1.5, -2.0, -3.0, -4.0, -6.0])


def pack_weight(w, fmt):
    k, n = w.shape
    w = f64(np.asarray(w, np.float32).astype(ml_dtypes.bfloat16)).reshape(k // 32, 32, n)
    amax = np.abs(w).max(1)
    if fmt == "e4m3":
        byte = np.frexp(amax)[1] - 1 + 127 - 7
    else:
        mant, ex = np.frexp(amax / 6.0)
        byte = np.where(mant > 0.5, ex, ex - 1) + 127
    byte = np.clip(np.where(amax > 0, byte, 1), 1, 254)
    scaled = (w * np.exp2(127.0 - byte)[:, None, :]).reshape(k, n).astype(np.float32)
    by_word = np.ascontiguousarray(scaled.reshape(k // 512, 128, 4, n).transpose(0, 1, 3, 2))
    if fmt == "e4m3":
        words = by_word.astype(ml_dtypes.float8_e4m3fn).view(np.uint8)
    else:
        c = by_word.astype(ml_dtypes.float4_e2m1fn).view(np.uint8) & 0xF
        words = (c[..., 0::2] | (c[..., 1::2] << 4)).reshape(k // 512, 128, 2 * n)
    return np.ascontiguousarray(words), np.ascontiguousarray(byte.astype(np.uint8).reshape(k // 512, 16, n))


def unpack_weight(words, scales, fmt):
    g, _, n = scales.shape
    words = np.ascontiguousarray(words).reshape(g, 128, n, -1)
    if fmt == "e4m3":
        vals = words.view(ml_dtypes.float8_e4m3fn).astype(np.float64)
    else:
        nib = np.empty((g, 128, n, 4), np.uint8)
        nib[..., 0::2] = words & 0xF
        nib[..., 1::2] = words >> 4
        vals = E2M1[nib]
    vals = vals * np.repeat(np.exp2(scales.astype(np.float64) - 127.0), 8, axis=1)[..., None]
    return vals.transpose(0, 1, 3, 2).reshape(g * 512, n)


def gelu(v):
    return 0.5 * v * (1.0 + np.tanh(np.sqrt(2.0 / np.pi) * (v + 0.044715 * v**3)))


def striped8(idx):
    return np.concatenate([v.reshape(-1, 16).T for v in idx]).astype(np.uint16)


def unstriped8(offs):
    return np.stack([offs[16 * g:16 * g + 16].T.reshape(-1) for g in range(8)]).astype(np.int64)


def runs(v, idx8):
    k = np.arange(v.shape[0])
    return v[k[:, None], idx8[k % 512 // 64]]


K, L, H, T, S, T2 = 1024, 512, 1024, 2048, 1024, 2048

def setup_inputs():
    n = np.random.standard_normal
    s = mx_kscale(K)[:, None]
    s2 = mx_kscale(L)[:, None]
    u = mx_kscale(H)[:, None]
    tab_words, tab_scales = pack_weight(n((K, T)) * s, "e4m3")
    tab2_words, tab2_scales = pack_weight(n((L, T)) * s2, "e4m3")
    w2_words, w2_scales = pack_weight(0.34 * n((L, H)) / np.sqrt(L) / s2, "e2m1")
    return {
        "tab_words": tab_words, "tab_scales": tab_scales,
        "offs": striped8(np.stack([np.random.permutation(T)[:S] for _ in range(8)])),
        "tab2_words": tab2_words, "tab2_scales": tab2_scales,
        "offs2": striped(np.random.permutation(T)[:S]),
        "w1": (n((K, H)) / np.sqrt(K) / s).astype(np.float32),
        "w2_words": w2_words, "w2_scales": w2_scales,
        "b2": np.random.uniform(-1.2, 1.2, H).astype(np.float32),
        "gain": (np.exp(0.4 * n(H)) * u[:, 0]).astype(np.float32),
        "w3": (3.0 * n((H, H)) / np.sqrt(H) / u).astype(np.float32),
        "page1": n((H, T2)).astype(np.float32),
        "wgo": np.exp(0.3 * n((128, S))).astype(np.float32),
        "offs3": striped(np.random.permutation(T2)[:S]),
    }

def reference(tab_words, tab_scales, offs, tab2_words, tab2_scales, offs2, w1, w2_words, w2_scales, b2, gain, w3, page1, wgo, offs3):
    v = runs(unpack_weight(tab_words, tab_scales, "e4m3"), unstriped8(offs))
    v2 = unpack_weight(tab2_words, tab2_scales, "e4m3")[:, unstriped(offs2)]
    w2 = unpack_weight(w2_words, w2_scales, "e2m1")
    a = mxq(f64(w1), 0, "e4m3").T @ v
    b = (w2.T @ v2) + f64(b2)[:, None]
    h = a * np.sin(b) * f64(gain)[:, None]
    e = mxq(f64(w3), 0, "e4m3").T @ mxq(h, 0, "e4m3")
    y = np.maximum(np.abs(a), e)
    out = f64(page1).copy()
    out[:, unstriped(offs3)] = np.tile(f64(wgo), (H // 128, 1)) * y
    return out

@@ -1,0 +1,264 @@
+import math
+from contextlib import ExitStack
+
+import concourse.mybir as mybir
+
+K, L, H, T, S, T2 = 1024, 512, 1024, 2048, 1024, 2048
+FLOPS = 2 * S * H * (K + L + H)
+
+F32 = mybir.dt.float32
+BF16 = mybir.dt.bfloat16
+I32 = mybir.dt.int32
+U32 = mybir.dt.uint32
+U16 = mybir.dt.uint16
+U8 = mybir.dt.uint8
+FP8X4 = mybir.dt.float8_e4m3fn_x4
+FP4X4 = mybir.dt.float4_e2m1fn_x4
+ACT = mybir.ActivationFunctionType
+ALU = mybir.AluOpType
+
+P = 128
+PACK = 4
+KP = P * PACK
+HALVES = H // KP
+CHUNKS = [(0, 512), (512, 512)]
+A_COLS = 128
+TAB_PLANE = 8
+SLABS = 11
+GS_BUFS = 3
+
+
+def tile_list_crease_fatigue_features_kernel(
+    tc, tab_words, tab_scales, offs, tab2_words, tab2_scales, offs2, w1, w2_words, w2_scales,
+    b2, gain, w3, page1, wgo, offs3, out,
+):
+    nc = tc.nc
+    with ExitStack() as ctx:
+        lists = ctx.enter_context(tc.tile_pool(name="lists", bufs=1))
+        keep = ctx.enter_context(tc.tile_pool(name="keep", bufs=1))
+        ring = ctx.enter_context(tc.tile_pool(name="ring", bufs=1))
+        psum = ctx.enter_context(tc.psum_pool(name="psum", bufs=1))
+
+        def slab(shape, dtype, name):
+            return ring.tile(shape, dtype, name=name, tag="slab", bufs=SLABS, align_bytes=64)
+
+        def words_of(dram, a):
+            return dram[a].rearrange("p t i -> p (t i)").bitcast(I32)
+
+        tab2_scale_win = keep.tile([P, T], U8, align_bytes=64)
+        w2_scale_raw = keep.tile([P, H], U8, align_bytes=64)
+        tab_scale_win = keep.tile([P, T], U8, align_bytes=64)
+        for plane in (tab2_scale_win, w2_scale_raw, tab_scale_win):
+            nc.vector.memset(plane[:].bitcast(I32), 0)
+
+        offs2_sb = lists.tile([P, S // 16], U16)
+        nc.sync.dma_start(offs2_sb[:], offs2)
+        tab2_win = slab([P, T], I32, "tab2_win")
+        nc.sync.dma_start(tab2_win[:], words_of(tab2_words, 0))
+        for d in range(4):
+            nc.sync.dma_start(tab2_scale_win[32 * d : 32 * d + 4, :].bitcast(I32), tab2_scales[0, 4 * d : 4 * d + 4, :].bitcast(I32))
+        w2_raw = keep.tile([P, 2 * H], U8, align_bytes=64)
+        nc.scalar.dma_start(w2_raw[:].bitcast(I32), w2_words[0].bitcast(I32))
+        for d in range(4):
+            nc.gpsimd.dma_start(w2_scale_raw[32 * d : 32 * d + 4, :].bitcast(I32), w2_scales[0, 4 * d : 4 * d + 4, :].bitcast(I32))
+        b2_sb = keep.tile([P, HALVES, PACK], F32)
+        gain_sb = keep.tile([P, HALVES, PACK], F32)
+        nc.scalar.dma_start(b2_sb[:], b2.rearrange("(b p t) -> p b t", p=P, t=PACK))
+        nc.scalar.dma_start(gain_sb[:], gain.rearrange("(b p t) -> p b t", p=P, t=PACK))
+        offs_sb = lists.tile([P, S // 16], U16)
+        nc.sync.dma_start(offs_sb[:], offs)
+        scale_rows = tab_scales.rearrange("a (g e) t -> e g a t", e=2)
+        for e in range(2):
+            nc.sync.dma_start(tab_scale_win[e:P:TAB_PLANE, :].bitcast(I32), scale_rows[e].bitcast(I32))
+        tab_win = []
+        for a in range(K // KP):
+            win = slab([P, T], I32, f"tab_win{a}")
+            nc.sync.dma_start(win[:], words_of(tab_words, a))
+            tab_win.append(win)
+
+        def load_weight(w, name, a, b):
+            raw = slab([P, PACK, KP], F32, f"{name}_raw{a}{b}")
+            nc.sync.dma_start(raw[:], w[KP * a : KP * (a + 1), KP * b : KP * (b + 1)].rearrange("(p j) c -> p j c", j=PACK))
+            return raw
+
+        def quantise_weight(raw, name, cast):
+            grouped = ring.tile([P, KP, PACK], BF16, name="grouped", tag="grouped", bufs=3, align_bytes=64)
+            cast(grouped[:].rearrange("p (t m) j -> p m j t", t=PACK), raw[:].rearrange("p j (m t) -> p m j t", t=PACK))
+            codes = keep.tile([P, KP], U32, name=f"{name}_codes", align_bytes=64)
+            scales = keep.tile([P, KP], U8, name=f"{name}_scales", align_bytes=64)
+            nc.vector.quantize_mx(out=codes[:].bitcast(FP8X4), scales=scales[:], in_=grouped[:].rearrange("p c j -> p (c j)"))
+            return codes, scales
+
+        w1_raw = {(a, b): load_weight(w1, "w1", a, b) for b in range(HALVES) for a in range(K // KP)}
+        w3_raw = {(a, 0): load_weight(w3, "w3", a, 0) for a in range(HALVES)}
+        offs3_sb = lists.tile([P, S // 16], U16)
+        nc.sync.dma_start(offs3_sb[:], offs3)
+
+        wgo_rows = wgo.rearrange("(m t) s -> m t s", t=PACK)
+        page_rows = page1.rearrange("(b p t) c -> b t p c", p=P, t=PACK)
+        out_rows = out.rearrange("(b p t) c -> b t p c", p=P, t=PACK)
+        wgo_sb = {}
+        pages = {}
+
+        def load_wgo(c):
+            j0, width = CHUNKS[c]
+            wgo_sb[c] = keep.tile([P, PACK, width], F32, name=f"wgo{c}")
+            for d in range(4):
+                nc.sync.dma_start(wgo_sb[c][32 * d : 32 * (d + 1), :, :], wgo_rows[:, :, j0 : j0 + width])
+
+        def load_page(b, t):
+            pages[b, t] = slab([P, T2], F32, f"page{b}{t}")
+            nc.sync.dma_start(pages[b, t][:], page_rows[b, t])
+
+        load_wgo(0)
+        load_page(0, 0)
+        load_page(0, 1)
+        for a in range(HALVES):
+            w3_raw[a, 1] = load_weight(w3, "w3", a, 1)
+        load_page(0, 2)
+        load_page(0, 3)
+        for t in range(PACK):
+            load_page(1, t)
+        for c in range(1, len(CHUNKS)):
+            load_wgo(c)
+
+        sin_bias = keep.tile([P, HALVES, PACK], F32)
+        nc.gpsimd.tensor_scalar(sin_bias[:], b2_sb[:], 0.5, -math.pi / 4, op0=ALU.mult, op1=ALU.add)
+        minus_two_gain = keep.tile([P, HALVES, PACK], F32)
+        nc.gpsimd.tensor_scalar(minus_two_gain[:], gain_sb[:], -2.0, 0.0, op0=ALU.mult, op1=ALU.add)
+
+        w2_codes = keep.tile([P, 2 * H], U8, align_bytes=64)
+        nc.scalar.copy(
+            w2_codes[:].bitcast(U16).rearrange("p (b t m) -> p b t m", b=HALVES, t=PACK),
+            w2_raw[:].bitcast(U16).rearrange("p (b m t) -> p b t m", b=HALVES, t=PACK),
+        )
+        w2_plane = keep.tile([P, H], U8, align_bytes=64)
+        nc.vector.tensor_copy(
+            w2_plane[:].rearrange("p (b t m) -> p b t m", b=HALVES, t=PACK),
+            w2_scale_raw[:].rearrange("p (b m t) -> p b t m", b=HALVES, t=PACK),
+        )
+
+        def gather_words(win, offsets, c, name):
+            j0, width = CHUNKS[c]
+            picked = keep.tile([P, width], U32, name=name, align_bytes=64)
+            nc.vector.tensor_copy(picked[:], win[:].bitcast(U32).indirect(offsets[:, j0 // 16 : (j0 + width) // 16]))
+            return picked
+
+        def gather_tab2(c):
+            j0, width = CHUNKS[c]
+            plane = keep.tile([P, width], U8, name=f"v2_plane{c}", align_bytes=64)
+            nc.vector.tensor_copy(plane[:], tab2_scale_win[:].indirect(offs2_sb[:, j0 // 16 : (j0 + width) // 16]))
+            return gather_words(tab2_win, offs2_sb, c, f"v2_words{c}"), plane
+
+        def gained_sine(c, b, v2):
+            width = CHUNKS[c][1]
+            words, plane = v2
+            gs = ring.tile([P, PACK, width], F32, name="gs", tag="gs", bufs=GS_BUFS)
+            for t in range(PACK):
+                col = KP * b + P * t
+                bank = psum.tile([P, width], F32, name="b_bank", tag="b_bank", bufs=2)
+                nc.tensor.matmul_mx(
+                    out=bank[:], lhsT=w2_codes[:, 2 * col : 2 * (col + P)].bitcast(FP4X4), lhsT_scale=w2_plane[:, col : col + P],
+                    rhs=words[:].bitcast(FP8X4), rhs_scale=plane[:], start=True, stop=True,
+                )
+                nc.scalar.activation(gs[:, t, :], bank[:], ACT.Sin, bias=sin_bias[:, b, t : t + 1], scale=0.5)
+            nc.scalar.activation(gs[:], gs[:], ACT.Square)
+            for t in range(PACK):
+                nc.scalar.activation(
+                    gs[:, t, :], gs[:, t, :], ACT.Identity, bias=gain_sb[:, b, t : t + 1], scale=minus_two_gain[:, b, t : t + 1]
+                )
+            return gs
+
+        v2 = {0: gather_tab2(0)}
+        gs = {(0, b): gained_sine(0, b, v2[0]) for b in range(HALVES)}
+
+        picked_scales = keep.tile([P, S], U8, align_bytes=64)
+        nc.vector.tensor_copy(picked_scales[:], tab_scale_win[:].indirect(offs_sb[:]))
+        v_planes = keep.tile([P, S], U8, align_bytes=64)
+        nc.vector.tensor_copy(v_planes[:].bitcast(I32), picked_scales[:].bitcast(I32))
+        for a in range(K // KP):
+            for e in range(2):
+                row = TAB_PLANE * a + e
+                nc.scalar.dma_start(v_planes[row + 2 : P : 32, :].bitcast(I32), picked_scales[row + 16 : P : 32, :].bitcast(I32))
+
+        v_words = {}
+        for a in range(K // KP):
+            v_words[0, a] = gather_words(tab_win[a], offs_sb, 0, f"v_words0{a}")
+
+        w1_q = {key: quantise_weight(raw, f"w1_{key[0]}{key[1]}", nc.vector.tensor_copy) for key, raw in w1_raw.items()}
+
+        def first_stage(c, b):
+            j0, width = CHUNKS[c]
+            abs_a = ring.tile([P, PACK, width], F32, name="abs_a", tag="abs_a", bufs=4)
+            h = ring.tile([P, width, PACK], BF16, name="h", tag="grouped", bufs=3, align_bytes=64)
+            for x0 in range(0, width, A_COLS):
+                bank = psum.tile([P, PACK, A_COLS], F32, name="a_bank", tag="a_bank", bufs=3)
+                for t in range(PACK):
+                    for a in range(K // KP):
+                        codes, scales = w1_q[a, b]
+                        nc.tensor.matmul_mx(
+                            out=bank[:, t, :], lhsT=codes[:, P * t : P * (t + 1)].bitcast(FP8X4), lhsT_scale=scales[:, P * t : P * (t + 1)],
+                            rhs=v_words[c, a][:, x0 : x0 + A_COLS].bitcast(FP8X4),
+                            rhs_scale=v_planes[TAB_PLANE * a : P, j0 + x0 : j0 + x0 + A_COLS],
+                            start=(a == 0), stop=(a == K // KP - 1),
+                        )
+                nc.vector.tensor_tensor(
+                    h[:, x0 : x0 + A_COLS, :].rearrange("p (c i) t -> p c t i", i=4),
+                    bank[:].rearrange("p t (c i) -> p c t i", i=4),
+                    gs[c, b][:, :, x0 : x0 + A_COLS].rearrange("p t (c i) -> p c t i", i=4),
+                    ALU.mult,
+                )
+                nc.scalar.activation(abs_a[:, :, x0 : x0 + A_COLS], bank[:], ACT.Abs)
+            codes = keep.tile([P, width], U32, name=f"h_codes{c}{b}", align_bytes=64)
+            scales = keep.tile([P, width], U8, name=f"h_scales{c}{b}", align_bytes=64)
+            nc.vector.quantize_mx(out=codes[:].bitcast(FP8X4), scales=scales[:], in_=h[:].rearrange("p c t -> p (c t)"))
+            return abs_a, (codes, scales)
+
+        abs_a, h_q = {}, {}
+        for b in range(HALVES):
+            abs_a[0, b], h_q[0, b] = first_stage(0, b)
+        w3_q = {(a, 0): quantise_weight(w3_raw[a, 0], f"w3_{a}0", nc.scalar.copy) for a in range(HALVES)}
+
+        def larger(c, b, t):
+            width = CHUNKS[c][1]
+            bank = psum.tile([P, width], F32, name="e_bank", tag="e_bank", bufs=3)
+            for a in range(HALVES):
+                codes, scales = w3_q[a, b]
+                h_codes, h_scales = h_q[c, a]
+                nc.tensor.matmul_mx(
+                    out=bank[:], lhsT=codes[:, P * t : P * (t + 1)].bitcast(FP8X4), lhsT_scale=scales[:, P * t : P * (t + 1)],
+                    rhs=h_codes[:].bitcast(FP8X4), rhs_scale=h_scales[:], start=(a == 0), stop=(a == HALVES - 1),
+                )
+            nc.vector.tensor_tensor(abs_a[c, b][:, t, :], bank[:], abs_a[c, b][:, t, :], ALU.max)
+
+        def place(c, b, t):
+            j0, width = CHUNKS[c]
+            nc.vector.tensor_tensor(
+                pages[b, t][:].indirect(offs3_sb[:, j0 // 16 : (j0 + width) // 16]), abs_a[c, b][:, t, :], wgo_sb[c][:, t, :], ALU.mult
+            )
+            if c == len(CHUNKS) - 1:
+                nc.sync.dma_start(out_rows[b, t], pages[b, t][:])
+
+        tiles = [(b, t) for b in range(HALVES) for t in range(PACK)]
+        waiting = None
+        for c in range(len(CHUNKS)):
+            for n, (b, t) in enumerate(tiles):
+                if c == 0 and n == 1:
+                    for a in range(HALVES):
+                        w3_q[a, 1] = quantise_weight(w3_raw[a, 1], f"w3_{a}1", nc.scalar.copy)
+                if c + 1 < len(CHUNKS):
+                    if n == 0:
+                        v2[c + 1] = gather_tab2(c + 1)
+                        for a in range(K // KP):
+                            v_words[c + 1, a] = gather_words(tab_win[a], offs_sb, c + 1, f"v_words{c + 1}{a}")
+                    if n in (2, 4):
+                        nb = n // 2 - 1
+                        gs[c + 1, nb] = gained_sine(c + 1, nb, v2[c + 1])
+                    if n in (4, 6):
+                        nb = n // 2 - 2
+                        abs_a[c + 1, nb], h_q[c + 1, nb] = first_stage(c + 1, nb)
+                larger(c, b, t)
+                if waiting is not None:
+                    place(*waiting)
+                waiting = (c, b, t)
+        place(*waiting)

@@ -25,7 +25,6 @@ CHUNKS = [(0, 512), (512, 512)]
 A_COLS = 128
 TAB_PLANE = 8
 SLABS = 11
-GS_BUFS = 3
 
 
 def tile_list_crease_fatigue_features_kernel(
@@ -45,51 +44,62 @@ def tile_list_crease_fatigue_features_kernel(
         def words_of(dram, a):
             return dram[a].rearrange("p t i -> p (t i)").bitcast(I32)
 
-        tab2_scale_win = keep.tile([P, T], U8, align_bytes=64)
-        w2_scale_raw = keep.tile([P, H], U8, align_bytes=64)
-        tab_scale_win = keep.tile([P, T], U8, align_bytes=64)
-        for plane in (tab2_scale_win, w2_scale_raw, tab_scale_win):
-            nc.vector.memset(plane[:].bitcast(I32), 0)
-
-        offs2_sb = lists.tile([P, S // 16], U16)
-        nc.sync.dma_start(offs2_sb[:], offs2)
-        tab2_win = slab([P, T], I32, "tab2_win")
-        nc.sync.dma_start(tab2_win[:], words_of(tab2_words, 0))
-        for d in range(4):
-            nc.sync.dma_start(tab2_scale_win[32 * d : 32 * d + 4, :].bitcast(I32), tab2_scales[0, 4 * d : 4 * d + 4, :].bitcast(I32))
-        w2_raw = keep.tile([P, 2 * H], U8, align_bytes=64)
-        nc.scalar.dma_start(w2_raw[:].bitcast(I32), w2_words[0].bitcast(I32))
-        for d in range(4):
-            nc.gpsimd.dma_start(w2_scale_raw[32 * d : 32 * d + 4, :].bitcast(I32), w2_scales[0, 4 * d : 4 * d + 4, :].bitcast(I32))
-        b2_sb = keep.tile([P, HALVES, PACK], F32)
-        gain_sb = keep.tile([P, HALVES, PACK], F32)
-        nc.scalar.dma_start(b2_sb[:], b2.rearrange("(b p t) -> p b t", p=P, t=PACK))
-        nc.scalar.dma_start(gain_sb[:], gain.rearrange("(b p t) -> p b t", p=P, t=PACK))
-        offs_sb = lists.tile([P, S // 16], U16)
-        nc.sync.dma_start(offs_sb[:], offs)
-        scale_rows = tab_scales.rearrange("a (g e) t -> e g a t", e=2)
-        for e in range(2):
-            nc.sync.dma_start(tab_scale_win[e:P:TAB_PLANE, :].bitcast(I32), scale_rows[e].bitcast(I32))
-        tab_win = []
-        for a in range(K // KP):
-            win = slab([P, T], I32, f"tab_win{a}")
-            nc.sync.dma_start(win[:], words_of(tab_words, a))
-            tab_win.append(win)
-
         def load_weight(w, name, a, b):
             raw = slab([P, PACK, KP], F32, f"{name}_raw{a}{b}")
             nc.sync.dma_start(raw[:], w[KP * a : KP * (a + 1), KP * b : KP * (b + 1)].rearrange("(p j) c -> p j c", j=PACK))
             return raw
 
-        def quantise_weight(raw, name, cast):
-            grouped = ring.tile([P, KP, PACK], BF16, name="grouped", tag="grouped", bufs=3, align_bytes=64)
+        def load_plane(plane, rows):
+            for d in range(4):
+                quadrant = rows[4 * d : 4 * d + 4, :].bitcast(I32)
+                nc.sync.dma_start(plane[32 * d : 32 * (d + 1), :].bitcast(I32), quadrant.unsqueeze(0).to_broadcast([8, *quadrant.shape]))
+
+        def load_table(words, a, name):
+            win = slab([P, T], I32, name)
+            nc.sync.dma_start(win[:], words_of(words, a))
+            return win
+
+        tab2_scale_win = keep.tile([P, T], U8, align_bytes=64)
+        w2_scale_raw = keep.tile([P, H], U8, align_bytes=64)
+        tab_scale_win = keep.tile([P, T], U8, align_bytes=64)
+        nc.gpsimd.memset(tab_scale_win[:].bitcast(I32), 0)
+
+        scale_rows = tab_scales.rearrange("a (g e) t -> e g a t", e=2)
+        for e in range(2):
+            nc.scalar.dma_start(tab_scale_win[e:P:TAB_PLANE, :].bitcast(I32), scale_rows[e].bitcast(I32))
+
+        offs2_sb = lists.tile([P, S // 16], U16)
+        nc.sync.dma_start(offs2_sb[:], offs2)
+        load_plane(w2_scale_raw, w2_scales[0])
+        load_plane(tab2_scale_win, tab2_scales[0])
+        offs_sb = lists.tile([P, S // 16], U16)
+        nc.sync.dma_start(offs_sb[:], offs)
+        w2_raw = keep.tile([P, 2 * H], U8, align_bytes=64)
+        nc.sync.dma_start(w2_raw[:].bitcast(I32), w2_words[0].bitcast(I32))
+        tab2_win = load_table(tab2_words, 0, "tab2_win")
+        b2_sb = keep.tile([P, HALVES, PACK], F32)
+        gain_sb = keep.tile([P, HALVES, PACK], F32)
+        nc.sync.dma_start(b2_sb[:], b2.rearrange("(b p t) -> p b t", p=P, t=PACK))
+        w1_raw = {(0, 0): load_weight(w1, "w1", 0, 0)}
+        tab_win = [load_table(tab_words, 0, "tab_win0")]
+        nc.sync.dma_start(gain_sb[:], gain.rearrange("(b p t) -> p b t", p=P, t=PACK))
+        w1_raw[1, 0] = load_weight(w1, "w1", 1, 0)
+        tab_win.append(load_table(tab_words, 1, "tab_win1"))
+        for a in range(K // KP):
+            w1_raw[a, 1] = load_weight(w1, "w1", a, 1)
+
+        def rounded_tile(width, tag):
+            bufs = 2 if tag == "early" else 1
+            return ring.tile([P, width, PACK], BF16, name=tag, tag=tag, bufs=bufs, align_bytes=64)
+
+        def quantise_weight(raw, name, cast, tag="early"):
+            grouped = rounded_tile(KP, tag)
             cast(grouped[:].rearrange("p (t m) j -> p m j t", t=PACK), raw[:].rearrange("p j (m t) -> p m j t", t=PACK))
             codes = keep.tile([P, KP], U32, name=f"{name}_codes", align_bytes=64)
             scales = keep.tile([P, KP], U8, name=f"{name}_scales", align_bytes=64)
             nc.vector.quantize_mx(out=codes[:].bitcast(FP8X4), scales=scales[:], in_=grouped[:].rearrange("p c j -> p (c j)"))
             return codes, scales
 
-        w1_raw = {(a, b): load_weight(w1, "w1", a, b) for b in range(HALVES) for a in range(K // KP)}
         w3_raw = {(a, 0): load_weight(w3, "w3", a, 0) for a in range(HALVES)}
         offs3_sb = lists.tile([P, S // 16], U16)
         nc.sync.dma_start(offs3_sb[:], offs3)
@@ -123,9 +133,9 @@ def tile_list_crease_fatigue_features_kernel(
             load_wgo(c)
 
         sin_bias = keep.tile([P, HALVES, PACK], F32)
-        nc.gpsimd.tensor_scalar(sin_bias[:], b2_sb[:], 0.5, -math.pi / 4, op0=ALU.mult, op1=ALU.add)
+        nc.scalar.activation(sin_bias[:], b2_sb[:], ACT.Copy, bias=-math.pi / 4, scale=0.5)
         minus_two_gain = keep.tile([P, HALVES, PACK], F32)
-        nc.gpsimd.tensor_scalar(minus_two_gain[:], gain_sb[:], -2.0, 0.0, op0=ALU.mult, op1=ALU.add)
+        nc.scalar.activation(minus_two_gain[:], gain_sb[:], ACT.Copy, scale=-2.0)
 
         w2_codes = keep.tile([P, 2 * H], U8, align_bytes=64)
         nc.scalar.copy(
@@ -140,7 +150,7 @@ def tile_list_crease_fatigue_features_kernel(
 
         def gather_words(win, offsets, c, name):
             j0, width = CHUNKS[c]
-            picked = keep.tile([P, width], U32, name=name, align_bytes=64)
+            picked = ring.tile([P, width], U32, name=name, tag=name, bufs=1, align_bytes=64)
             nc.vector.tensor_copy(picked[:], win[:].bitcast(U32).indirect(offsets[:, j0 // 16 : (j0 + width) // 16]))
             return picked
 
@@ -150,19 +160,19 @@ def tile_list_crease_fatigue_features_kernel(
             nc.vector.tensor_copy(plane[:], tab2_scale_win[:].indirect(offs2_sb[:, j0 // 16 : (j0 + width) // 16]))
             return gather_words(tab2_win, offs2_sb, c, f"v2_words{c}"), plane
 
-        def gained_sine(c, b, v2):
+        def gained_sine(c, b, v2, both):
             width = CHUNKS[c][1]
             words, plane = v2
-            gs = ring.tile([P, PACK, width], F32, name="gs", tag="gs", bufs=GS_BUFS)
+            gs = both[:, b]
             for t in range(PACK):
                 col = KP * b + P * t
-                bank = psum.tile([P, width], F32, name="b_bank", tag="b_bank", bufs=2)
+                bank = psum.tile([P, width], F32, name="b_bank", tag="bank", bufs=8)
                 nc.tensor.matmul_mx(
                     out=bank[:], lhsT=w2_codes[:, 2 * col : 2 * (col + P)].bitcast(FP4X4), lhsT_scale=w2_plane[:, col : col + P],
                     rhs=words[:].bitcast(FP8X4), rhs_scale=plane[:], start=True, stop=True,
                 )
                 nc.scalar.activation(gs[:, t, :], bank[:], ACT.Sin, bias=sin_bias[:, b, t : t + 1], scale=0.5)
-            nc.scalar.activation(gs[:], gs[:], ACT.Square)
+            nc.scalar.activation(gs, gs, ACT.Square)
             for t in range(PACK):
                 nc.scalar.activation(
                     gs[:, t, :], gs[:, t, :], ACT.Identity, bias=gain_sb[:, b, t : t + 1], scale=minus_two_gain[:, b, t : t + 1]
@@ -170,29 +180,32 @@ def tile_list_crease_fatigue_features_kernel(
             return gs
 
         v2 = {0: gather_tab2(0)}
-        gs = {(0, b): gained_sine(0, b, v2[0]) for b in range(HALVES)}
+        w1_q = {}
+        both = ring.tile([P, HALVES, PACK, CHUNKS[0][1]], F32, name="gs", tag="gs", bufs=1)
+        gs = {(0, b): gained_sine(0, b, v2[0], both) for b in range(HALVES)}
 
         picked_scales = keep.tile([P, S], U8, align_bytes=64)
         nc.vector.tensor_copy(picked_scales[:], tab_scale_win[:].indirect(offs_sb[:]))
         v_planes = keep.tile([P, S], U8, align_bytes=64)
         nc.vector.tensor_copy(v_planes[:].bitcast(I32), picked_scales[:].bitcast(I32))
-        for a in range(K // KP):
-            for e in range(2):
-                row = TAB_PLANE * a + e
-                nc.scalar.dma_start(v_planes[row + 2 : P : 32, :].bitcast(I32), picked_scales[row + 16 : P : 32, :].bitcast(I32))
+        for e in range(2):
+            nc.scalar.dma_start(
+                v_planes[e + 2 : P - 16 : TAB_PLANE, :].bitcast(I32), picked_scales[e + 16 : P : TAB_PLANE, :].bitcast(I32)
+            )
 
         v_words = {}
         for a in range(K // KP):
-            v_words[0, a] = gather_words(tab_win[a], offs_sb, 0, f"v_words0{a}")
+            v_words[0, a] = gather_words(tab_win[a], offs_sb, 0, f"v_words{a}")
 
-        w1_q = {key: quantise_weight(raw, f"w1_{key[0]}{key[1]}", nc.vector.tensor_copy) for key, raw in w1_raw.items()}
+        for a, b in ((0, 0), (1, 0), (0, 1), (1, 1)):
+            w1_q[a, b] = quantise_weight(w1_raw[a, b], f"w1_{a}{b}", nc.vector.tensor_copy, "h0" if (a, b) == (1, 1) else "early")
 
         def first_stage(c, b):
             j0, width = CHUNKS[c]
             abs_a = ring.tile([P, PACK, width], F32, name="abs_a", tag="abs_a", bufs=4)
-            h = ring.tile([P, width, PACK], BF16, name="h", tag="grouped", bufs=3, align_bytes=64)
+            h = rounded_tile(width, f"h{b}")
             for x0 in range(0, width, A_COLS):
-                bank = psum.tile([P, PACK, A_COLS], F32, name="a_bank", tag="a_bank", bufs=3)
+                bank = psum.tile([P, PACK, A_COLS], F32, name="a_bank", tag="bank", bufs=8)
                 for t in range(PACK):
                     for a in range(K // KP):
                         codes, scales = w1_q[a, b]
@@ -202,26 +215,29 @@ def tile_list_crease_fatigue_features_kernel(
                             rhs_scale=v_planes[TAB_PLANE * a : P, j0 + x0 : j0 + x0 + A_COLS],
                             start=(a == 0), stop=(a == K // KP - 1),
                         )
+                if c > 0:
+                    nc.scalar.activation(abs_a[:, :, x0 : x0 + A_COLS], bank[:], ACT.Abs)
                 nc.vector.tensor_tensor(
                     h[:, x0 : x0 + A_COLS, :].rearrange("p (c i) t -> p c t i", i=4),
                     bank[:].rearrange("p t (c i) -> p c t i", i=4),
                     gs[c, b][:, :, x0 : x0 + A_COLS].rearrange("p t (c i) -> p c t i", i=4),
                     ALU.mult,
                 )
-                nc.scalar.activation(abs_a[:, :, x0 : x0 + A_COLS], bank[:], ACT.Abs)
+                if c == 0:
+                    nc.scalar.activation(abs_a[:, :, x0 : x0 + A_COLS], bank[:], ACT.Abs)
             codes = keep.tile([P, width], U32, name=f"h_codes{c}{b}", align_bytes=64)
             scales = keep.tile([P, width], U8, name=f"h_scales{c}{b}", align_bytes=64)
             nc.vector.quantize_mx(out=codes[:].bitcast(FP8X4), scales=scales[:], in_=h[:].rearrange("p c t -> p (c t)"))
             return abs_a, (codes, scales)
 
         abs_a, h_q = {}, {}
-        for b in range(HALVES):
-            abs_a[0, b], h_q[0, b] = first_stage(0, b)
         w3_q = {(a, 0): quantise_weight(w3_raw[a, 0], f"w3_{a}0", nc.scalar.copy) for a in range(HALVES)}
+        abs_a[0, 0], h_q[0, 0] = first_stage(0, 0)
+        abs_a[0, 1], h_q[0, 1] = first_stage(0, 1)
 
         def larger(c, b, t):
             width = CHUNKS[c][1]
-            bank = psum.tile([P, width], F32, name="e_bank", tag="e_bank", bufs=3)
+            bank = psum.tile([P, width], F32, name="e_bank", tag="bank", bufs=8)
             for a in range(HALVES):
                 codes, scales = w3_q[a, b]
                 h_codes, h_scales = h_q[c, a]
@@ -229,12 +245,17 @@ def tile_list_crease_fatigue_features_kernel(
                     out=bank[:], lhsT=codes[:, P * t : P * (t + 1)].bitcast(FP8X4), lhsT_scale=scales[:, P * t : P * (t + 1)],
                     rhs=h_codes[:].bitcast(FP8X4), rhs_scale=h_scales[:], start=(a == 0), stop=(a == HALVES - 1),
                 )
-            nc.vector.tensor_tensor(abs_a[c, b][:, t, :], bank[:], abs_a[c, b][:, t, :], ALU.max)
+            if c + 1 < len(CHUNKS) and (b, t) == (HALVES - 1, PACK - 1):
+                y = ring.tile([P, width], F32, name="y", tag="h1", bufs=1, align_bytes=64)[:]
+            else:
+                y = abs_a[c, b][:, t, :]
+            nc.vector.tensor_tensor(y, bank[:], abs_a[c, b][:, t, :], ALU.max)
+            return y
 
-        def place(c, b, t):
+        def place(c, b, t, y):
             j0, width = CHUNKS[c]
             nc.vector.tensor_tensor(
-                pages[b, t][:].indirect(offs3_sb[:, j0 // 16 : (j0 + width) // 16]), abs_a[c, b][:, t, :], wgo_sb[c][:, t, :], ALU.mult
+                pages[b, t][:].indirect(offs3_sb[:, j0 // 16 : (j0 + width) // 16]), y, wgo_sb[c][:, t, :], ALU.mult
             )
             if c == len(CHUNKS) - 1:
                 nc.sync.dma_start(out_rows[b, t], pages[b, t][:])
@@ -245,20 +266,21 @@ def tile_list_crease_fatigue_features_kernel(
             for n, (b, t) in enumerate(tiles):
                 if c == 0 and n == 1:
                     for a in range(HALVES):
-                        w3_q[a, 1] = quantise_weight(w3_raw[a, 1], f"w3_{a}1", nc.scalar.copy)
+                        w3_q[a, 1] = quantise_weight(w3_raw[a, 1], f"w3_{a}1", nc.scalar.copy, "h1")
                 if c + 1 < len(CHUNKS):
                     if n == 0:
+                        both = ring.tile([P, HALVES, PACK, CHUNKS[c + 1][1]], F32, name="gs", tag="gs", bufs=1)
                         v2[c + 1] = gather_tab2(c + 1)
                         for a in range(K // KP):
-                            v_words[c + 1, a] = gather_words(tab_win[a], offs_sb, c + 1, f"v_words{c + 1}{a}")
+                            v_words[c + 1, a] = gather_words(tab_win[a], offs_sb, c + 1, f"v_words{a}")
                     if n in (2, 4):
                         nb = n // 2 - 1
-                        gs[c + 1, nb] = gained_sine(c + 1, nb, v2[c + 1])
+                        gs[c + 1, nb] = gained_sine(c + 1, nb, v2[c + 1], both)
                     if n in (4, 6):
                         nb = n // 2 - 2
                         abs_a[c + 1, nb], h_q[c + 1, nb] = first_stage(c + 1, nb)
-                larger(c, b, t)
+                y = larger(c, b, t)
                 if waiting is not None:
                     place(*waiting)
-                waiting = (c, b, t)
+                waiting = (c, b, t, y)
         place(*waiting)

import math
from contextlib import ExitStack

import concourse.mybir as mybir

K, L, H, T, S, T2 = 1024, 512, 1024, 2048, 1024, 2048
FLOPS = 2 * S * H * (K + L + H)

F32 = mybir.dt.float32
BF16 = mybir.dt.bfloat16
I32 = mybir.dt.int32
U32 = mybir.dt.uint32
U16 = mybir.dt.uint16
U8 = mybir.dt.uint8
FP8X4 = mybir.dt.float8_e4m3fn_x4
FP4X4 = mybir.dt.float4_e2m1fn_x4
ACT = mybir.ActivationFunctionType
ALU = mybir.AluOpType

P = 128
PACK = 4
KP = P * PACK
HALVES = H // KP
CHUNKS = [(0, 512), (512, 512)]
A_COLS = 128
TAB_PLANE = 8
SLABS = 11


def tile_list_crease_fatigue_features_kernel(
    tc, tab_words, tab_scales, offs, tab2_words, tab2_scales, offs2, w1, w2_words, w2_scales,
    b2, gain, w3, page1, wgo, offs3, out,
):
    nc = tc.nc
    with ExitStack() as ctx:
        lists = ctx.enter_context(tc.tile_pool(name="lists", bufs=1))
        keep = ctx.enter_context(tc.tile_pool(name="keep", bufs=1))
        ring = ctx.enter_context(tc.tile_pool(name="ring", bufs=1))
        psum = ctx.enter_context(tc.psum_pool(name="psum", bufs=1))

        def slab(shape, dtype, name):
            return ring.tile(shape, dtype, name=name, tag="slab", bufs=SLABS, align_bytes=64)

        def words_of(dram, a):
            return dram[a].rearrange("p t i -> p (t i)").bitcast(I32)

        def load_weight(w, name, a, b):
            raw = slab([P, PACK, KP], F32, f"{name}_raw{a}{b}")
            nc.sync.dma_start(raw[:], w[KP * a : KP * (a + 1), KP * b : KP * (b + 1)].rearrange("(p j) c -> p j c", j=PACK))
            return raw

        def load_plane(plane, rows):
            for d in range(4):
                quadrant = rows[4 * d : 4 * d + 4, :].bitcast(I32)
                nc.sync.dma_start(plane[32 * d : 32 * (d + 1), :].bitcast(I32), quadrant.unsqueeze(0).to_broadcast([8, *quadrant.shape]))

        def load_table(words, a, name):
            win = slab([P, T], I32, name)
            nc.sync.dma_start(win[:], words_of(words, a))
            return win

        tab2_scale_win = keep.tile([P, T], U8, align_bytes=64)
        w2_scale_raw = keep.tile([P, H], U8, align_bytes=64)
        tab_scale_win = keep.tile([P, T], U8, align_bytes=64)
        nc.gpsimd.memset(tab_scale_win[:].bitcast(I32), 0)

        scale_rows = tab_scales.rearrange("a (g e) t -> e g a t", e=2)
        for e in range(2):
            nc.scalar.dma_start(tab_scale_win[e:P:TAB_PLANE, :].bitcast(I32), scale_rows[e].bitcast(I32))

        offs2_sb = lists.tile([P, S // 16], U16)
        nc.sync.dma_start(offs2_sb[:], offs2)
        load_plane(w2_scale_raw, w2_scales[0])
        load_plane(tab2_scale_win, tab2_scales[0])
        offs_sb = lists.tile([P, S // 16], U16)
        nc.sync.dma_start(offs_sb[:], offs)
        w2_raw = keep.tile([P, 2 * H], U8, align_bytes=64)
        nc.sync.dma_start(w2_raw[:].bitcast(I32), w2_words[0].bitcast(I32))
        tab2_win = load_table(tab2_words, 0, "tab2_win")
        b2_sb = keep.tile([P, HALVES, PACK], F32)
        gain_sb = keep.tile([P, HALVES, PACK], F32)
        nc.sync.dma_start(b2_sb[:], b2.rearrange("(b p t) -> p b t", p=P, t=PACK))
        w1_raw = {(0, 0): load_weight(w1, "w1", 0, 0)}
        tab_win = [load_table(tab_words, 0, "tab_win0")]
        nc.sync.dma_start(gain_sb[:], gain.rearrange("(b p t) -> p b t", p=P, t=PACK))
        w1_raw[1, 0] = load_weight(w1, "w1", 1, 0)
        tab_win.append(load_table(tab_words, 1, "tab_win1"))
        for a in range(K // KP):
            w1_raw[a, 1] = load_weight(w1, "w1", a, 1)

        def rounded_tile(width, tag):
            bufs = 2 if tag == "early" else 1
            return ring.tile([P, width, PACK], BF16, name=tag, tag=tag, bufs=bufs, align_bytes=64)

        def quantise_weight(raw, name, cast, tag="early"):
            grouped = rounded_tile(KP, tag)
            cast(grouped[:].rearrange("p (t m) j -> p m j t", t=PACK), raw[:].rearrange("p j (m t) -> p m j t", t=PACK))
            codes = keep.tile([P, KP], U32, name=f"{name}_codes", align_bytes=64)
            scales = keep.tile([P, KP], U8, name=f"{name}_scales", align_bytes=64)
            nc.vector.quantize_mx(out=codes[:].bitcast(FP8X4), scales=scales[:], in_=grouped[:].rearrange("p c j -> p (c j)"))
            return codes, scales

        w3_raw = {(a, 0): load_weight(w3, "w3", a, 0) for a in range(HALVES)}
        offs3_sb = lists.tile([P, S // 16], U16)
        nc.sync.dma_start(offs3_sb[:], offs3)

        wgo_rows = wgo.rearrange("(m t) s -> m t s", t=PACK)
        page_rows = page1.rearrange("(b p t) c -> b t p c", p=P, t=PACK)
        out_rows = out.rearrange("(b p t) c -> b t p c", p=P, t=PACK)
        wgo_sb = {}
        pages = {}

        def load_wgo(c):
            j0, width = CHUNKS[c]
            wgo_sb[c] = keep.tile([P, PACK, width], F32, name=f"wgo{c}")
            for d in range(4):
                nc.sync.dma_start(wgo_sb[c][32 * d : 32 * (d + 1), :, :], wgo_rows[:, :, j0 : j0 + width])

        def load_page(b, t):
            pages[b, t] = slab([P, T2], F32, f"page{b}{t}")
            nc.sync.dma_start(pages[b, t][:], page_rows[b, t])

        load_wgo(0)
        load_page(0, 0)
        load_page(0, 1)
        for a in range(HALVES):
            w3_raw[a, 1] = load_weight(w3, "w3", a, 1)
        load_page(0, 2)
        load_page(0, 3)
        for t in range(PACK):
            load_page(1, t)
        for c in range(1, len(CHUNKS)):
            load_wgo(c)

        sin_bias = keep.tile([P, HALVES, PACK], F32)
        nc.scalar.activation(sin_bias[:], b2_sb[:], ACT.Copy, bias=-math.pi / 4, scale=0.5)
        minus_two_gain = keep.tile([P, HALVES, PACK], F32)
        nc.scalar.activation(minus_two_gain[:], gain_sb[:], ACT.Copy, scale=-2.0)

        w2_codes = keep.tile([P, 2 * H], U8, align_bytes=64)
        nc.scalar.copy(
            w2_codes[:].bitcast(U16).rearrange("p (b t m) -> p b t m", b=HALVES, t=PACK),
            w2_raw[:].bitcast(U16).rearrange("p (b m t) -> p b t m", b=HALVES, t=PACK),
        )
        w2_plane = keep.tile([P, H], U8, align_bytes=64)
        nc.vector.tensor_copy(
            w2_plane[:].rearrange("p (b t m) -> p b t m", b=HALVES, t=PACK),
            w2_scale_raw[:].rearrange("p (b m t) -> p b t m", b=HALVES, t=PACK),
        )

        def gather_words(win, offsets, c, name):
            j0, width = CHUNKS[c]
            picked = ring.tile([P, width], U32, name=name, tag=name, bufs=1, align_bytes=64)
            nc.vector.tensor_copy(picked[:], win[:].bitcast(U32).indirect(offsets[:, j0 // 16 : (j0 + width) // 16]))
            return picked

        def gather_tab2(c):
            j0, width = CHUNKS[c]
            plane = keep.tile([P, width], U8, name=f"v2_plane{c}", align_bytes=64)
            nc.vector.tensor_copy(plane[:], tab2_scale_win[:].indirect(offs2_sb[:, j0 // 16 : (j0 + width) // 16]))
            return gather_words(tab2_win, offs2_sb, c, f"v2_words{c}"), plane

        def gained_sine(c, b, v2, both):
            width = CHUNKS[c][1]
            words, plane = v2
            gs = both[:, b]
            for t in range(PACK):
                col = KP * b + P * t
                bank = psum.tile([P, width], F32, name="b_bank", tag="bank", bufs=8)
                nc.tensor.matmul_mx(
                    out=bank[:], lhsT=w2_codes[:, 2 * col : 2 * (col + P)].bitcast(FP4X4), lhsT_scale=w2_plane[:, col : col + P],
                    rhs=words[:].bitcast(FP8X4), rhs_scale=plane[:], start=True, stop=True,
                )
                nc.scalar.activation(gs[:, t, :], bank[:], ACT.Sin, bias=sin_bias[:, b, t : t + 1], scale=0.5)
            nc.scalar.activation(gs, gs, ACT.Square)
            for t in range(PACK):
                nc.scalar.activation(
                    gs[:, t, :], gs[:, t, :], ACT.Identity, bias=gain_sb[:, b, t : t + 1], scale=minus_two_gain[:, b, t : t + 1]
                )
            return gs

        v2 = {0: gather_tab2(0)}
        w1_q = {}
        both = ring.tile([P, HALVES, PACK, CHUNKS[0][1]], F32, name="gs", tag="gs", bufs=1)
        gs = {(0, b): gained_sine(0, b, v2[0], both) for b in range(HALVES)}

        picked_scales = keep.tile([P, S], U8, align_bytes=64)
        nc.vector.tensor_copy(picked_scales[:], tab_scale_win[:].indirect(offs_sb[:]))
        v_planes = keep.tile([P, S], U8, align_bytes=64)
        nc.vector.tensor_copy(v_planes[:].bitcast(I32), picked_scales[:].bitcast(I32))
        for e in range(2):
            nc.scalar.dma_start(
                v_planes[e + 2 : P - 16 : TAB_PLANE, :].bitcast(I32), picked_scales[e + 16 : P : TAB_PLANE, :].bitcast(I32)
            )

        v_words = {}
        for a in range(K // KP):
            v_words[0, a] = gather_words(tab_win[a], offs_sb, 0, f"v_words{a}")

        for a, b in ((0, 0), (1, 0), (0, 1), (1, 1)):
            w1_q[a, b] = quantise_weight(w1_raw[a, b], f"w1_{a}{b}", nc.vector.tensor_copy, "h0" if (a, b) == (1, 1) else "early")

        def first_stage(c, b):
            j0, width = CHUNKS[c]
            abs_a = ring.tile([P, PACK, width], F32, name="abs_a", tag="abs_a", bufs=4)
            h = rounded_tile(width, f"h{b}")
            for x0 in range(0, width, A_COLS):
                bank = psum.tile([P, PACK, A_COLS], F32, name="a_bank", tag="bank", bufs=8)
                for t in range(PACK):
                    for a in range(K // KP):
                        codes, scales = w1_q[a, b]
                        nc.tensor.matmul_mx(
                            out=bank[:, t, :], lhsT=codes[:, P * t : P * (t + 1)].bitcast(FP8X4), lhsT_scale=scales[:, P * t : P * (t + 1)],
                            rhs=v_words[c, a][:, x0 : x0 + A_COLS].bitcast(FP8X4),
                            rhs_scale=v_planes[TAB_PLANE * a : P, j0 + x0 : j0 + x0 + A_COLS],
                            start=(a == 0), stop=(a == K // KP - 1),
                        )
                if c > 0:
                    nc.scalar.activation(abs_a[:, :, x0 : x0 + A_COLS], bank[:], ACT.Abs)
                nc.vector.tensor_tensor(
                    h[:, x0 : x0 + A_COLS, :].rearrange("p (c i) t -> p c t i", i=4),
                    bank[:].rearrange("p t (c i) -> p c t i", i=4),
                    gs[c, b][:, :, x0 : x0 + A_COLS].rearrange("p t (c i) -> p c t i", i=4),
                    ALU.mult,
                )
                if c == 0:
                    nc.scalar.activation(abs_a[:, :, x0 : x0 + A_COLS], bank[:], ACT.Abs)
            codes = keep.tile([P, width], U32, name=f"h_codes{c}{b}", align_bytes=64)
            scales = keep.tile([P, width], U8, name=f"h_scales{c}{b}", align_bytes=64)
            nc.vector.quantize_mx(out=codes[:].bitcast(FP8X4), scales=scales[:], in_=h[:].rearrange("p c t -> p (c t)"))
            return abs_a, (codes, scales)

        abs_a, h_q = {}, {}
        w3_q = {(a, 0): quantise_weight(w3_raw[a, 0], f"w3_{a}0", nc.scalar.copy) for a in range(HALVES)}
        abs_a[0, 0], h_q[0, 0] = first_stage(0, 0)
        abs_a[0, 1], h_q[0, 1] = first_stage(0, 1)

        def larger(c, b, t):
            width = CHUNKS[c][1]
            bank = psum.tile([P, width], F32, name="e_bank", tag="bank", bufs=8)
            for a in range(HALVES):
                codes, scales = w3_q[a, b]
                h_codes, h_scales = h_q[c, a]
                nc.tensor.matmul_mx(
                    out=bank[:], lhsT=codes[:, P * t : P * (t + 1)].bitcast(FP8X4), lhsT_scale=scales[:, P * t : P * (t + 1)],
                    rhs=h_codes[:].bitcast(FP8X4), rhs_scale=h_scales[:], start=(a == 0), stop=(a == HALVES - 1),
                )
            if c + 1 < len(CHUNKS) and (b, t) == (HALVES - 1, PACK - 1):
                y = ring.tile([P, width], F32, name="y", tag="h1", bufs=1, align_bytes=64)[:]
            else:
                y = abs_a[c, b][:, t, :]
            nc.vector.tensor_tensor(y, bank[:], abs_a[c, b][:, t, :], ALU.max)
            return y

        def place(c, b, t, y):
            j0, width = CHUNKS[c]
            nc.vector.tensor_tensor(
                pages[b, t][:].indirect(offs3_sb[:, j0 // 16 : (j0 + width) // 16]), y, wgo_sb[c][:, t, :], ALU.mult
            )
            if c == len(CHUNKS) - 1:
                nc.sync.dma_start(out_rows[b, t], pages[b, t][:])

        tiles = [(b, t) for b in range(HALVES) for t in range(PACK)]
        waiting = None
        for c in range(len(CHUNKS)):
            for n, (b, t) in enumerate(tiles):
                if c == 0 and n == 1:
                    for a in range(HALVES):
                        w3_q[a, 1] = quantise_weight(w3_raw[a, 1], f"w3_{a}1", nc.scalar.copy, "h1")
                if c + 1 < len(CHUNKS):
                    if n == 0:
                        both = ring.tile([P, HALVES, PACK, CHUNKS[c + 1][1]], F32, name="gs", tag="gs", bufs=1)
                        v2[c + 1] = gather_tab2(c + 1)
                        for a in range(K // KP):
                            v_words[c + 1, a] = gather_words(tab_win[a], offs_sb, c + 1, f"v_words{a}")
                    if n in (2, 4):
                        nb = n // 2 - 1
                        gs[c + 1, nb] = gained_sine(c + 1, nb, v2[c + 1], both)
                    if n in (4, 6):
                        nb = n // 2 - 2
                        abs_a[c + 1, nb], h_q[c + 1, nb] = first_stage(c + 1, nb)
                y = larger(c, b, t)
                if waiting is not None:
                    place(*waiting)
                waiting = (c, b, t, y)
        place(*waiting)
